import numpy as np
import ml_dtypes


def mxq(x, axis, fmt="e4m3"):
    dtype, down = {"e4m3": (ml_dtypes.float8_e4m3fn, 7), "e5m2": (ml_dtypes.float8_e5m2, 14)}[fmt]
    v = np.moveaxis(np.asarray(x, np.float32).astype(ml_dtypes.bfloat16).astype(np.float64), axis, -1)
    blocks = v.reshape(v.shape[:-1] + (-1, 32))
    amax = np.abs(blocks).max(-1, keepdims=True)
    byte = np.maximum(np.where(amax > 0, np.frexp(amax)[1] - 1 + 127, 0) - down, 1)
    scale = np.exp2(byte - 127.0)
    codes = (blocks / scale).astype(np.float32).astype(dtype).astype(np.float64)
    return np.moveaxis((codes * scale).reshape(v.shape), -1, axis)


WIDE = False


def mx_kscale(k):
    if not WIDE:
        return np.ones(k)
    levels = np.array([30, -30])
    if k % 512:
        return np.exp2(np.random.permutation(np.resize(levels, k // 32))).repeat(32)
    a = np.empty((k // 512, 16))
    for p in range(k // 512):
        a[p, :8] = np.random.permutation(np.resize(levels, 8))
        for g in range(8):
            far = levels[np.abs(levels - a[p, g]) >= 10]
            a[p, g + 8] = far[np.random.randint(len(far))]
    return np.exp2(a.ravel()).repeat(32)


def f64(x):
    return np.asarray(x).astype(np.float64)


def striped(idx):
    return np.tile(np.asarray(idx).reshape(-1, 16).T, (8, 1)).astype(np.uint16)


def unstriped(offs):
    return offs[:16].T.reshape(-1).astype(np.int64)


E2M1 = np.array([0.0, 0.5, 1.0, 1.5, 2.0, 3.0, 4.0, 6.0, -0.0, -0.5, -1.0, -1.5, -2.0, -3.0, -4.0, -6.0])


def pack_weight(w, fmt):
    k, n = w.shape
    w = f64(np.asarray(w, np.float32).astype(ml_dtypes.bfloat16)).reshape(k // 32, 32, n)
    amax = np.abs(w).max(1)
    if fmt == "e4m3":
        byte = np.frexp(amax)[1] - 1 + 127 - 7
    else:
        mant, ex = np.frexp(amax / 6.0)
        byte = np.where(mant > 0.5, ex, ex - 1) + 127
    byte = np.clip(np.where(amax > 0, byte, 1), 1, 254)
    scaled = (w * np.exp2(127.0 - byte)[:, None, :]).reshape(k, n).astype(np.float32)
    by_word = np.ascontiguousarray(scaled.reshape(k // 512, 128, 4, n).transpose(0, 1, 3, 2))
    if fmt == "e4m3":
        words = by_word.astype(ml_dtypes.float8_e4m3fn).view(np.uint8)
    else:
        c = by_word.astype(ml_dtypes.float4_e2m1fn).view(np.uint8) & 0xF
        words = (c[..., 0::2] | (c[..., 1::2] << 4)).reshape(k // 512, 128, 2 * n)
    return np.ascontiguousarray(words), np.ascontiguousarray(byte.astype(np.uint8).reshape(k // 512, 16, n))


def unpack_weight(words, scales, fmt):
    g, _, n = scales.shape
    words = np.ascontiguousarray(words).reshape(g, 128, n, -1)
    if fmt == "e4m3":
        vals = words.view(ml_dtypes.float8_e4m3fn).astype(np.float64)
    else:
        nib = np.empty((g, 128, n, 4), np.uint8)
        nib[..., 0::2] = words & 0xF
        nib[..., 1::2] = words >> 4
        vals = E2M1[nib]
    vals = vals * np.repeat(np.exp2(scales.astype(np.float64) - 127.0), 8, axis=1)[..., None]
    return vals.transpose(0, 1, 3, 2).reshape(g * 512, n)


K, T, I, J, N, Z, S, C, E = 512, 1024, 512, 256, 256, 1024, 1024, 512, 1024


def setup_inputs():
    n = np.random.standard_normal
    idx = np.random.permutation(T)[:I]
    idx2 = np.random.permutation(Z)[:J]
    idx3 = np.random.permutation(Z)[:J]
    idx4 = np.random.permutation(C)[:J]
    idx5 = np.random.permutation(C)[:J]
    idx6 = np.random.permutation(S)[:N]
    idx7 = np.random.permutation(E)[:J]
    fk = mx_kscale(K)
    fi = mx_kscale(I)
    ti = np.ones(T)
    ti[idx] = fi
    xkp = pack_weight(n((K, T)) * 0.3 * fk[:, None] * ti, "e2m1")
    xqp = pack_weight(n((K, Z)) * 0.3 / fk[:, None], "e4m3")
    vsp = pack_weight(n((I, S)) / fi[:, None], "e4m3")
    return {
        "xk_words": xkp[0],
        "xk_scales": xkp[1],
        "xq_words": xqp[0],
        "xq_scales": xqp[1],
        "vs_words": vsp[0],
        "vs_scales": vsp[1],
        "offs": striped(idx),
        "offs2": striped(idx2),
        "offs3": striped(idx3),
        "offs4": striped(idx4),
        "offs5": striped(idx5),
        "offs6": striped(idx6),
        "offs7": striped(idx7),
    }


def reference(xk_words, xk_scales, xq_words, xq_scales, vs_words, vs_scales, offs, offs2, offs3, offs4, offs5, offs6, offs7):
    idx = unstriped(offs)
    idx2 = unstriped(offs2)
    idx3 = unstriped(offs3)
    idx4 = unstriped(offs4)
    idx5 = unstriped(offs5)
    idx6 = unstriped(offs6)
    idx7 = unstriped(offs7)
    xku = unpack_weight(xk_words, xk_scales, "e2m1")
    xqu = unpack_weight(xq_words, xq_scales, "e4m3")
    vsu = unpack_weight(vs_words, vs_scales, "e4m3")
    xkidxg = xku[:, idx]
    xqidx2g = xqu[:, idx2]
    s1 = xkidxg.T @ xqidx2g
    xqidx3g = xqu[:, idx3]
    s2 = xkidxg.T @ xqidx3g
    pw = np.zeros((I, C))
    pw[:, idx4] = s1
    hid = np.abs(pw[:, idx5] - s2)
    vsidx6g = vsu[:, idx6]
    hidq = mxq(hid, 0, "e5m2")
    p = vsidx6g.T @ hidq
    y = np.zeros((N, E))
    y[:, idx7] = p
    return y

@@ -1,0 +1,207 @@
+from contextlib import ExitStack
+
+import concourse.mybir as mybir
+
+F32 = mybir.dt.float32
+BF16 = mybir.dt.bfloat16
+I32 = mybir.dt.int32
+U32 = mybir.dt.uint32
+U16 = mybir.dt.uint16
+U8 = mybir.dt.uint8
+E4M3 = mybir.dt.float8_e4m3fn_x4
+E5M2 = mybir.dt.float8_e5m2_x4
+E2M1 = mybir.dt.float4_e2m1fn_x4
+ACT = mybir.ActivationFunctionType
+ALU = mybir.AluOpType
+
+P = 128
+PACK = 4
+K, T, I, J, N, Z, S, C, E = 512, 1024, 512, 256, 256, 1024, 1024, 512, 1024
+FLOPS = 2 * (2 * K * I * J + I * N * J)
+
+
+def tile_list_contest_twice_board_scattered_kernel(
+    tc, xk_words, xk_scales, xq_words, xq_scales, vs_words, vs_scales,
+    offs, offs2, offs3, offs4, offs5, offs6, offs7, out,
+):
+    nc = tc.nc
+    with ExitStack() as ctx:
+        lists = ctx.enter_context(tc.tile_pool(name="lists", bufs=1))
+        sb = ctx.enter_context(tc.tile_pool(name="sb", bufs=1))
+        psum = ctx.enter_context(tc.psum_pool(name="psum", bufs=1))
+
+        def load_list(src, name):
+            tile = lists.tile(list(src.shape), U16, name=name)
+            nc.sync.dma_start(tile[:], src)
+            return tile
+
+        def zeroed_scale_window(width, name):
+            tile = sb.tile([P, width], U8, name=name, align_bytes=64)
+            nc.gpsimd.memset(tile[:].bitcast(I32), 0)
+            return tile
+
+        def load_scale_rows(tile, src):
+            for q in range(4):
+                nc.sync.dma_start(
+                    tile[32 * q : 32 * q + 4, :].bitcast(I32), src[0, 4 * q : 4 * q + 4, :].bitcast(I32)
+                )
+
+        def load_words(src_bytes, width, dtype, name):
+            tile = sb.tile([P, width], dtype, name=name, align_bytes=64)
+            nc.sync.dma_start(tile[:].bitcast(I32), src_bytes.bitcast(I32))
+            return tile
+
+        def gather(window, offsets, count, dtype, name):
+            tile = sb.tile([P, count], dtype, name=name, align_bytes=64)
+            nc.vector.tensor_copy(tile[:], window[:].indirect(offsets[:]))
+            return tile
+
+        xk_s = zeroed_scale_window(T, "xk_s")
+        xq_s = zeroed_scale_window(Z, "xq_s")
+        boards = []
+        for t in range(PACK):
+            board = sb.tile([P, C], F32, name="board%d" % t)
+            nc.gpsimd.memset(board[:], 0.0)
+            boards.append(board)
+        vs_s = zeroed_scale_window(S, "vs_s")
+
+        o1 = load_list(offs, "o1")
+        xk_w = load_words(xk_words[0], T, U16, "xk_w")
+        load_scale_rows(xk_s, xk_scales)
+        o2 = load_list(offs2, "o2")
+        xq_w = load_words(xq_words[0].rearrange("p c r -> p (c r)"), Z, U32, "xq_w")
+        load_scale_rows(xq_s, xq_scales)
+        o3 = load_list(offs3, "o3")
+        o4 = load_list(offs4, "o4")
+        o6 = load_list(offs6, "o6")
+        vs_w = load_words(vs_words[0].rearrange("p c r -> p (c r)"), S, U32, "vs_w")
+        load_scale_rows(vs_s, vs_scales)
+        o5 = load_list(offs5, "o5")
+        o7 = load_list(offs7, "o7")
+
+        key_w = gather(xk_w, o1, I, U16, "key_w")
+        key_s = gather(xk_s, o1, I, U8, "key_s")
+        dealt_w = sb.tile([P, I], U16, name="dealt_w", align_bytes=64)
+        nc.vector.tensor_copy(
+            dealt_w[:].rearrange("p (t c i) -> p c t i", t=PACK, i=8),
+            key_w[:].rearrange("p (c i t) -> p c t i", t=PACK, i=8),
+        )
+        q1_w = gather(xq_w, o2, J, U32, "q1_w")
+        dealt_s = sb.tile([P, I], U8, name="dealt_s", align_bytes=64)
+        nc.vector.tensor_copy(
+            dealt_s[:].rearrange("p (t c i) -> p c t i", t=PACK, i=16),
+            key_s[:].rearrange("p (c i t) -> p c t i", t=PACK, i=16),
+        )
+        q1_s = gather(xq_s, o2, J, U8, "q1_s")
+
+        def scores(acc, t, q_w, q_s):
+            cols = slice(P * t, P * (t + 1))
+            nc.tensor.matmul_mx(
+                out=acc,
+                lhsT=dealt_w[:, cols].bitcast(E2M1), lhsT_scale=dealt_s[:, cols],
+                rhs=q_w[:].bitcast(E4M3), rhs_scale=q_s[:],
+                start=True, stop=True,
+            )
+
+        s1 = {}
+        for t in range(PACK):
+            s1[t] = psum.tile([P, J], F32, name="s1_%d" % t, tag="bank%d" % t)
+            scores(s1[t][:], t, q1_w, q1_s)
+
+        q2_w = gather(xq_w, o3, J, U32, "q2_w")
+        q2_s = gather(xq_s, o3, J, U8, "q2_s")
+        s2 = []
+        for u in range(2):
+            acc = psum.tile([P, 2, J], F32, name="s2_%d" % u)
+            for v in range(2):
+                scores(acc[:, v, :], 2 * u + v, q2_w, q2_s)
+            s2.append(acc)
+
+        def stage(on_vector, acc, width, name):
+            staged = sb.tile([P, width], F32, name=name)
+            if on_vector:
+                nc.vector.tensor_copy(staged[:], acc[:])
+            else:
+                nc.scalar.copy(staged[:], acc[:])
+            return staged
+
+        def put(on_vector, window, offsets, staged):
+            if on_vector:
+                nc.vector.tensor_copy(window[:].indirect(offsets), staged[:])
+            else:
+                nc.scalar.activation(window[:].indirect(offsets), staged[:], ACT.Copy)
+
+        a0 = stage(False, s1[0], J, "a0")
+        put(False, boards[0], o4[:], a0)
+        a2 = stage(False, s1[2], J, "a2")
+        a3 = stage(False, s1[3], J, "a3")
+        put(False, boards[2], o4[:], a2)
+        put(False, boards[3], o4[:], a3)
+        a1 = stage(True, s1[1], J, "a1")
+        val_w = gather(vs_w, o6, N, U32, "val_w")
+        put(True, boards[1], o4[:], a1)
+
+        H = J // 2
+        HC = H // 16
+        hid = [sb.tile([P, H, PACK], BF16, name="hid%d" % h, align_bytes=64) for h in range(2)]
+        diffs = [sb.tile([P, 2, J], F32, name="diff%d" % u) for u in range(2)]
+        picked = sb.tile([P, 2, J], F32, name="picked")
+
+        def magnitude(u, h):
+            nc.scalar.activation(
+                hid[h][:, :, 2 * u : 2 * u + 2],
+                diffs[u][:, :, H * h : H * (h + 1)].rearrange("p v j -> p j v"),
+                ACT.Abs,
+            )
+
+        for t in range(2):
+            nc.vector.tensor_copy(picked[:, t, :], boards[t][:].indirect(o5[:]))
+        late = sb.tile([P, J], F32, name="late2", tag="late")
+        nc.vector.tensor_copy(late[:], boards[2][:].indirect(o5[:]))
+        nc.vector.tensor_tensor(diffs[0][:], picked[:], s2[0][:], ALU.subtract)
+        nc.vector.tensor_tensor(diffs[1][:, 0, :], late[:], s2[1][:, 0, :], ALU.subtract)
+        late = sb.tile([P, J], F32, name="late3", tag="late")
+        for h in range(2):
+            magnitude(0, h)
+        for h in range(2):
+            nc.vector.tensor_copy(
+                late[:, H * h : H * (h + 1)], boards[3][:].indirect(o5[:, HC * h : HC * (h + 1)])
+            )
+        for h in range(2):
+            cols = slice(H * h, H * (h + 1))
+            nc.vector.tensor_tensor(diffs[1][:, 1, cols], late[:, cols], s2[1][:, 1, cols], ALU.subtract)
+        for h in range(2):
+            magnitude(1, h)
+        val_s = gather(vs_s, o6, N, U8, "val_s")
+
+        pages = []
+        for b in range(N // P):
+            page = sb.tile([P, E], F32, name="page%d" % b)
+            nc.vector.memset(page[:], 0.0)
+            pages.append(page)
+
+        staged = {}
+        for h in range(2):
+            hid_w = sb.tile([P, H], U32, name="hid_w%d" % h, align_bytes=64)
+            hid_s = sb.tile([P, H], U8, name="hid_s%d" % h, align_bytes=64)
+            nc.vector.quantize_mx(
+                out=hid_w[:].bitcast(E5M2), scales=hid_s[:], in_=hid[h][:].rearrange("p j t -> p (j t)")
+            )
+            for b in range(N // P):
+                cols = slice(P * b, P * (b + 1))
+                acc = psum.tile([P, H], F32, name="p%d%d" % (b, h), tag="bank%d" % (2 * h + b))
+                nc.tensor.matmul_mx(
+                    out=acc[:],
+                    lhsT=val_w[:, cols].bitcast(E4M3), lhsT_scale=val_s[:, cols],
+                    rhs=hid_w[:].bitcast(E5M2), rhs_scale=hid_s[:],
+                    start=True, stop=True,
+                )
+                staged[b, h] = acc
+        for h in range(2):
+            for b in range(N // P):
+                staged[b, h] = stage(b == 1, staged[b, h], H, "p_sb%d%d" % (b, h))
+        for h in range(2):
+            for b in range(N // P):
+                put(b == 1, pages[b], o7[:, HC * h : HC * (h + 1)], staged[b, h])
+        for b in range(N // P):
+            nc.sync.dma_start(out[P * b : P * (b + 1), :], pages[b][:])

@@ -36,7 +36,7 @@ def tile_list_contest_twice_board_scattered_kernel(
             return tile
 
         def zeroed_scale_window(width, name):
-            tile = sb.tile([P, width], U8, name=name, align_bytes=64)
+            tile = sb.tile([P, width], U8, name=name, tag=name, align_bytes=64)
             nc.gpsimd.memset(tile[:].bitcast(I32), 0)
             return tile
 
@@ -47,7 +47,7 @@ def tile_list_contest_twice_board_scattered_kernel(
                 )
 
         def load_words(src_bytes, width, dtype, name):
-            tile = sb.tile([P, width], dtype, name=name, align_bytes=64)
+            tile = sb.tile([P, width], dtype, name=name, tag=name, align_bytes=64)
             nc.sync.dma_start(tile[:].bitcast(I32), src_bytes.bitcast(I32))
             return tile
 
@@ -61,16 +61,16 @@ def tile_list_contest_twice_board_scattered_kernel(
         boards = []
         for t in range(PACK):
             board = sb.tile([P, C], F32, name="board%d" % t)
-            nc.gpsimd.memset(board[:], 0.0)
+            nc.vector.memset(board[:], 0.0)
             boards.append(board)
         vs_s = zeroed_scale_window(S, "vs_s")
 
         o1 = load_list(offs, "o1")
         xk_w = load_words(xk_words[0], T, U16, "xk_w")
         load_scale_rows(xk_s, xk_scales)
-        o2 = load_list(offs2, "o2")
         xq_w = load_words(xq_words[0].rearrange("p c r -> p (c r)"), Z, U32, "xq_w")
         load_scale_rows(xq_s, xq_scales)
+        o2 = load_list(offs2, "o2")
         o3 = load_list(offs3, "o3")
         o4 = load_list(offs4, "o4")
         o6 = load_list(offs6, "o6")
@@ -80,33 +80,46 @@ def tile_list_contest_twice_board_scattered_kernel(
         o7 = load_list(offs7, "o7")
 
         key_w = gather(xk_w, o1, I, U16, "key_w")
-        key_s = gather(xk_s, o1, I, U8, "key_s")
+        dealt_s = sb.tile([P, I], U8, name="dealt_s", align_bytes=64)
+        nc.vector.tensor_copy(dealt_s[:].rearrange("p (t q) -> p q t", t=PACK), xk_s[:].indirect(o1[:]))
         dealt_w = sb.tile([P, I], U16, name="dealt_w", align_bytes=64)
         nc.vector.tensor_copy(
             dealt_w[:].rearrange("p (t c i) -> p c t i", t=PACK, i=8),
             key_w[:].rearrange("p (c i t) -> p c t i", t=PACK, i=8),
         )
-        q1_w = gather(xq_w, o2, J, U32, "q1_w")
-        dealt_s = sb.tile([P, I], U8, name="dealt_s", align_bytes=64)
-        nc.vector.tensor_copy(
-            dealt_s[:].rearrange("p (t c i) -> p c t i", t=PACK, i=16),
-            key_s[:].rearrange("p (c i t) -> p c t i", t=PACK, i=16),
-        )
-        q1_s = gather(xq_s, o2, J, U8, "q1_s")
+        H = J // 2
+        HC = H // 16
+        q1_w = sb.tile([P, J], U32, name="q1_w", align_bytes=64)
+        q1_s = sb.tile([P, J], U8, name="q1_s", align_bytes=64)
+        for h in range(2):
+            nc.vector.tensor_copy(q1_w[:, H * h : H * (h + 1)], xq_w[:].indirect(o2[:, HC * h : HC * (h + 1)]))
+            nc.vector.tensor_copy(q1_s[:, H * h : H * (h + 1)], xq_s[:].indirect(o2[:, HC * h : HC * (h + 1)]))
 
         def scores(acc, t, q_w, q_s):
             cols = slice(P * t, P * (t + 1))
             nc.tensor.matmul_mx(
                 out=acc,
                 lhsT=dealt_w[:, cols].bitcast(E2M1), lhsT_scale=dealt_s[:, cols],
-                rhs=q_w[:].bitcast(E4M3), rhs_scale=q_s[:],
+                rhs=q_w.bitcast(E4M3), rhs_scale=q_s,
                 start=True, stop=True,
             )
 
-        s1 = {}
-        for t in range(PACK):
-            s1[t] = psum.tile([P, J], F32, name="s1_%d" % t, tag="bank%d" % t)
-            scores(s1[t][:], t, q1_w, q1_s)
+        def put(on_vector, window, offsets, staged):
+            if on_vector:
+                nc.vector.tensor_copy(window[:].indirect(offsets), staged)
+            else:
+                nc.scalar.activation(window[:].indirect(offsets), staged, ACT.Copy)
+
+        s1 = [psum.tile([P, J if t else H], F32, name="s1_%d" % t, tag="bank%d" % t) for t in range(PACK)]
+        scores(s1[0][:, 0:H], 0, q1_w[:, 0:H], q1_s[:, 0:H])
+        first = sb.tile([P, H], F32, name="first")
+        nc.scalar.copy(first[:], s1[0][:, 0:H])
+        put(False, boards[0], o4[:, 0:HC], first[:])
+        scores(s1[1][:], 1, q1_w[:], q1_s[:])
+        s1_late = psum.tile([P, H], F32, name="s1_late")
+        scores(s1_late[:], 0, q1_w[:, H:J], q1_s[:, H:J])
+        for t in (2, 3):
+            scores(s1[t][:], t, q1_w[:], q1_s[:])
 
         q2_w = gather(xq_w, o3, J, U32, "q2_w")
         q2_s = gather(xq_s, o3, J, U8, "q2_s")
@@ -114,7 +127,7 @@ def tile_list_contest_twice_board_scattered_kernel(
         for u in range(2):
             acc = psum.tile([P, 2, J], F32, name="s2_%d" % u)
             for v in range(2):
-                scores(acc[:, v, :], 2 * u + v, q2_w, q2_s)
+                scores(acc[:, v, :], 2 * u + v, q2_w[:], q2_s[:])
             s2.append(acc)
 
         def stage(on_vector, acc, width, name):
@@ -125,27 +138,21 @@ def tile_list_contest_twice_board_scattered_kernel(
                 nc.scalar.copy(staged[:], acc[:])
             return staged
 
-        def put(on_vector, window, offsets, staged):
-            if on_vector:
-                nc.vector.tensor_copy(window[:].indirect(offsets), staged[:])
-            else:
-                nc.scalar.activation(window[:].indirect(offsets), staged[:], ACT.Copy)
-
-        a0 = stage(False, s1[0], J, "a0")
-        put(False, boards[0], o4[:], a0)
+        a1 = sb.tile([P, J], F32, name="a1")
+        nc.vector.tensor_copy(a1[:], s1[1][:])
+        second = stage(False, s1_late, H, "second")
         a2 = stage(False, s1[2], J, "a2")
+        put(False, boards[0], o4[:, HC:], second[:])
         a3 = stage(False, s1[3], J, "a3")
-        put(False, boards[2], o4[:], a2)
-        put(False, boards[3], o4[:], a3)
-        a1 = stage(True, s1[1], J, "a1")
+        put(False, boards[2], o4[:], a2[:])
+        put(False, boards[3], o4[:], a3[:])
         val_w = gather(vs_w, o6, N, U32, "val_w")
-        put(True, boards[1], o4[:], a1)
+        put(True, boards[1], o4[:], a1[:])
+        val_s = gather(vs_s, o6, N, U8, "val_s")
 
-        H = J // 2
-        HC = H // 16
         hid = [sb.tile([P, H, PACK], BF16, name="hid%d" % h, align_bytes=64) for h in range(2)]
         diffs = [sb.tile([P, 2, J], F32, name="diff%d" % u) for u in range(2)]
-        picked = sb.tile([P, 2, J], F32, name="picked")
+        picked = [sb.tile([P, 2, J], F32, name="picked0"), sb.tile([P, 2, J], F32, name="picked1")]
 
         def magnitude(u, h):
             nc.scalar.activation(
@@ -154,30 +161,22 @@ def tile_list_contest_twice_board_scattered_kernel(
                 ACT.Abs,
             )
 
-        for t in range(2):
-            nc.vector.tensor_copy(picked[:, t, :], boards[t][:].indirect(o5[:]))
-        late = sb.tile([P, J], F32, name="late2", tag="late")
-        nc.vector.tensor_copy(late[:], boards[2][:].indirect(o5[:]))
-        nc.vector.tensor_tensor(diffs[0][:], picked[:], s2[0][:], ALU.subtract)
-        nc.vector.tensor_tensor(diffs[1][:, 0, :], late[:], s2[1][:, 0, :], ALU.subtract)
-        late = sb.tile([P, J], F32, name="late3", tag="late")
         for h in range(2):
-            magnitude(0, h)
-        for h in range(2):
-            nc.vector.tensor_copy(
-                late[:, H * h : H * (h + 1)], boards[3][:].indirect(o5[:, HC * h : HC * (h + 1)])
+            nc.scalar.activation(
+                picked[1][:, 1, H * h : H * (h + 1)], boards[3][:].indirect(o5[:, HC * h : HC * (h + 1)]), ACT.Copy
             )
+        for t in (1, 0, 2):
+            nc.vector.tensor_copy(picked[t // 2][:, t % 2, :], boards[t][:].indirect(o5[:]))
         for h in range(2):
             cols = slice(H * h, H * (h + 1))
-            nc.vector.tensor_tensor(diffs[1][:, 1, cols], late[:, cols], s2[1][:, 1, cols], ALU.subtract)
-        for h in range(2):
-            magnitude(1, h)
-        val_s = gather(vs_s, o6, N, U8, "val_s")
+            for u in range(2):
+                nc.vector.tensor_tensor(diffs[u][:, :, cols], picked[u][:, :, cols], s2[u][:, :, cols], ALU.subtract)
+                magnitude(u, h)
 
         pages = []
         for b in range(N // P):
-            page = sb.tile([P, E], F32, name="page%d" % b)
-            nc.vector.memset(page[:], 0.0)
+            page = sb.tile([P, E], F32, name="page%d" % b, tag=("xq_w", "xq_s")[b], align_bytes=64)
+            nc.gpsimd.memset(page[:], 0.0)
             pages.append(page)
 
         staged = {}
@@ -202,6 +201,6 @@ def tile_list_contest_twice_board_scattered_kernel(
                 staged[b, h] = stage(b == 1, staged[b, h], H, "p_sb%d%d" % (b, h))
         for h in range(2):
             for b in range(N // P):
-                put(b == 1, pages[b], o7[:, HC * h : HC * (h + 1)], staged[b, h])
+                put(b == 1, pages[b], o7[:, HC * h : HC * (h + 1)], staged[b, h][:])
         for b in range(N // P):
             nc.sync.dma_start(out[P * b : P * (b + 1), :], pages[b][:])

@@ -65,8 +65,8 @@ def tile_list_contest_twice_board_scattered_kernel(
             boards.append(board)
         vs_s = zeroed_scale_window(S, "vs_s")
 
-        o1 = load_list(offs, "o1")
         xk_w = load_words(xk_words[0], T, U16, "xk_w")
+        o1 = load_list(offs, "o1")
         load_scale_rows(xk_s, xk_scales)
         xq_w = load_words(xq_words[0].rearrange("p c r -> p (c r)"), Z, U32, "xq_w")
         load_scale_rows(xq_s, xq_scales)
@@ -196,11 +196,13 @@ def tile_list_contest_twice_board_scattered_kernel(
                     start=True, stop=True,
                 )
                 staged[b, h] = acc
-        for h in range(2):
-            for b in range(N // P):
-                staged[b, h] = stage(b == 1, staged[b, h], H, "p_sb%d%d" % (b, h))
-        for h in range(2):
-            for b in range(N // P):
-                put(b == 1, pages[b], o7[:, HC * h : HC * (h + 1)], staged[b, h][:])
+        p_sb = [sb.tile([P, J], F32, name="p_sb%d" % b) for b in range(N // P)]
+        nc.scalar.copy(p_sb[0][:, 0:H], staged[0, 0][:])
+        put(False, pages[0], o7[:, 0:HC], p_sb[0][:, 0:H])
+        nc.vector.tensor_copy(p_sb[1][:, 0:H], staged[1, 0][:])
+        nc.vector.tensor_copy(p_sb[0][:, H:], staged[0, 1][:])
+        put(False, pages[0], o7[:, HC:], p_sb[0][:, H:])
+        nc.vector.tensor_copy(p_sb[1][:, H:], staged[1, 1][:])
+        put(True, pages[1], o7[:], p_sb[1][:])
         for b in range(N // P):
             nc.sync.dma_start(out[P * b : P * (b + 1), :], pages[b][:])

@@ -63,6 +63,8 @@ def tile_list_contest_twice_board_scattered_kernel(
             board = sb.tile([P, C], F32, name="board%d" % t)
             nc.vector.memset(board[:], 0.0)
             boards.append(board)
+        page1 = sb.tile([P, E], F32, name="page1")
+        nc.vector.memset(page1[:], 0.0)
         vs_s = zeroed_scale_window(S, "vs_s")
 
         xk_w = load_words(xk_words[0], T, U16, "xk_w")
@@ -143,7 +145,8 @@ def tile_list_contest_twice_board_scattered_kernel(
         second = stage(False, s1_late, H, "second")
         a2 = stage(False, s1[2], J, "a2")
         put(False, boards[0], o4[:, HC:], second[:])
-        a3 = stage(False, s1[3], J, "a3")
+        a3 = sb.tile([P, J], F32, name="a3", tag="a3")
+        nc.scalar.copy(a3[:], s1[3][:])
         put(False, boards[2], o4[:], a2[:])
         put(False, boards[3], o4[:], a3[:])
         val_w = gather(vs_w, o6, N, U32, "val_w")
@@ -173,11 +176,9 @@ def tile_list_contest_twice_board_scattered_kernel(
                 nc.vector.tensor_tensor(diffs[u][:, :, cols], picked[u][:, :, cols], s2[u][:, :, cols], ALU.subtract)
                 magnitude(u, h)
 
-        pages = []
-        for b in range(N // P):
-            page = sb.tile([P, E], F32, name="page%d" % b, tag=("xq_w", "xq_s")[b], align_bytes=64)
-            nc.gpsimd.memset(page[:], 0.0)
-            pages.append(page)
+        page0 = sb.tile([P, E], F32, name="page0", tag="a3")
+        nc.gpsimd.memset(page0[:], 0.0)
+        pages = [page0, page1]
 
         staged = {}
         for h in range(2):

from contextlib import ExitStack

import concourse.mybir as mybir

F32 = mybir.dt.float32
BF16 = mybir.dt.bfloat16
I32 = mybir.dt.int32
U32 = mybir.dt.uint32
U16 = mybir.dt.uint16
U8 = mybir.dt.uint8
E4M3 = mybir.dt.float8_e4m3fn_x4
E5M2 = mybir.dt.float8_e5m2_x4
E2M1 = mybir.dt.float4_e2m1fn_x4
ACT = mybir.ActivationFunctionType
ALU = mybir.AluOpType

P = 128
PACK = 4
K, T, I, J, N, Z, S, C, E = 512, 1024, 512, 256, 256, 1024, 1024, 512, 1024
FLOPS = 2 * (2 * K * I * J + I * N * J)


def tile_list_contest_twice_board_scattered_kernel(
    tc, xk_words, xk_scales, xq_words, xq_scales, vs_words, vs_scales,
    offs, offs2, offs3, offs4, offs5, offs6, offs7, out,
):
    nc = tc.nc
    with ExitStack() as ctx:
        lists = ctx.enter_context(tc.tile_pool(name="lists", bufs=1))
        sb = ctx.enter_context(tc.tile_pool(name="sb", bufs=1))
        psum = ctx.enter_context(tc.psum_pool(name="psum", bufs=1))

        def load_list(src, name):
            tile = lists.tile(list(src.shape), U16, name=name)
            nc.sync.dma_start(tile[:], src)
            return tile

        def zeroed_scale_window(width, name):
            tile = sb.tile([P, width], U8, name=name, tag=name, align_bytes=64)
            nc.gpsimd.memset(tile[:].bitcast(I32), 0)
            return tile

        def load_scale_rows(tile, src):
            for q in range(4):
                nc.sync.dma_start(
                    tile[32 * q : 32 * q + 4, :].bitcast(I32), src[0, 4 * q : 4 * q + 4, :].bitcast(I32)
                )

        def load_words(src_bytes, width, dtype, name):
            tile = sb.tile([P, width], dtype, name=name, tag=name, align_bytes=64)
            nc.sync.dma_start(tile[:].bitcast(I32), src_bytes.bitcast(I32))
            return tile

        def gather(window, offsets, count, dtype, name):
            tile = sb.tile([P, count], dtype, name=name, align_bytes=64)
            nc.vector.tensor_copy(tile[:], window[:].indirect(offsets[:]))
            return tile

        xk_s = zeroed_scale_window(T, "xk_s")
        xq_s = zeroed_scale_window(Z, "xq_s")
        boards = []
        for t in range(PACK):
            board = sb.tile([P, C], F32, name="board%d" % t)
            nc.vector.memset(board[:], 0.0)
            boards.append(board)
        page1 = sb.tile([P, E], F32, name="page1")
        nc.vector.memset(page1[:], 0.0)
        vs_s = zeroed_scale_window(S, "vs_s")

        xk_w = load_words(xk_words[0], T, U16, "xk_w")
        o1 = load_list(offs, "o1")
        load_scale_rows(xk_s, xk_scales)
        xq_w = load_words(xq_words[0].rearrange("p c r -> p (c r)"), Z, U32, "xq_w")
        load_scale_rows(xq_s, xq_scales)
        o2 = load_list(offs2, "o2")
        o3 = load_list(offs3, "o3")
        o4 = load_list(offs4, "o4")
        o6 = load_list(offs6, "o6")
        vs_w = load_words(vs_words[0].rearrange("p c r -> p (c r)"), S, U32, "vs_w")
        load_scale_rows(vs_s, vs_scales)
        o5 = load_list(offs5, "o5")
        o7 = load_list(offs7, "o7")

        key_w = gather(xk_w, o1, I, U16, "key_w")
        dealt_s = sb.tile([P, I], U8, name="dealt_s", align_bytes=64)
        nc.vector.tensor_copy(dealt_s[:].rearrange("p (t q) -> p q t", t=PACK), xk_s[:].indirect(o1[:]))
        dealt_w = sb.tile([P, I], U16, name="dealt_w", align_bytes=64)
        nc.vector.tensor_copy(
            dealt_w[:].rearrange("p (t c i) -> p c t i", t=PACK, i=8),
            key_w[:].rearrange("p (c i t) -> p c t i", t=PACK, i=8),
        )
        H = J // 2
        HC = H // 16
        q1_w = sb.tile([P, J], U32, name="q1_w", align_bytes=64)
        q1_s = sb.tile([P, J], U8, name="q1_s", align_bytes=64)
        for h in range(2):
            nc.vector.tensor_copy(q1_w[:, H * h : H * (h + 1)], xq_w[:].indirect(o2[:, HC * h : HC * (h + 1)]))
            nc.vector.tensor_copy(q1_s[:, H * h : H * (h + 1)], xq_s[:].indirect(o2[:, HC * h : HC * (h + 1)]))

        def scores(acc, t, q_w, q_s):
            cols = slice(P * t, P * (t + 1))
            nc.tensor.matmul_mx(
                out=acc,
                lhsT=dealt_w[:, cols].bitcast(E2M1), lhsT_scale=dealt_s[:, cols],
                rhs=q_w.bitcast(E4M3), rhs_scale=q_s,
                start=True, stop=True,
            )

        def put(on_vector, window, offsets, staged):
            if on_vector:
                nc.vector.tensor_copy(window[:].indirect(offsets), staged)
            else:
                nc.scalar.activation(window[:].indirect(offsets), staged, ACT.Copy)

        s1 = [psum.tile([P, J if t else H], F32, name="s1_%d" % t, tag="bank%d" % t) for t in range(PACK)]
        scores(s1[0][:, 0:H], 0, q1_w[:, 0:H], q1_s[:, 0:H])
        first = sb.tile([P, H], F32, name="first")
        nc.scalar.copy(first[:], s1[0][:, 0:H])
        put(False, boards[0], o4[:, 0:HC], first[:])
        scores(s1[1][:], 1, q1_w[:], q1_s[:])
        s1_late = psum.tile([P, H], F32, name="s1_late")
        scores(s1_late[:], 0, q1_w[:, H:J], q1_s[:, H:J])
        for t in (2, 3):
            scores(s1[t][:], t, q1_w[:], q1_s[:])

        q2_w = gather(xq_w, o3, J, U32, "q2_w")
        q2_s = gather(xq_s, o3, J, U8, "q2_s")
        s2 = []
        for u in range(2):
            acc = psum.tile([P, 2, J], F32, name="s2_%d" % u)
            for v in range(2):
                scores(acc[:, v, :], 2 * u + v, q2_w[:], q2_s[:])
            s2.append(acc)

        def stage(on_vector, acc, width, name):
            staged = sb.tile([P, width], F32, name=name)
            if on_vector:
                nc.vector.tensor_copy(staged[:], acc[:])
            else:
                nc.scalar.copy(staged[:], acc[:])
            return staged

        a1 = sb.tile([P, J], F32, name="a1")
        nc.vector.tensor_copy(a1[:], s1[1][:])
        second = stage(False, s1_late, H, "second")
        a2 = stage(False, s1[2], J, "a2")
        put(False, boards[0], o4[:, HC:], second[:])
        a3 = sb.tile([P, J], F32, name="a3", tag="a3")
        nc.scalar.copy(a3[:], s1[3][:])
        put(False, boards[2], o4[:], a2[:])
        put(False, boards[3], o4[:], a3[:])
        val_w = gather(vs_w, o6, N, U32, "val_w")
        put(True, boards[1], o4[:], a1[:])
        val_s = gather(vs_s, o6, N, U8, "val_s")

        hid = [sb.tile([P, H, PACK], BF16, name="hid%d" % h, align_bytes=64) for h in range(2)]
        diffs = [sb.tile([P, 2, J], F32, name="diff%d" % u) for u in range(2)]
        picked = [sb.tile([P, 2, J], F32, name="picked0"), sb.tile([P, 2, J], F32, name="picked1")]

        def magnitude(u, h):
            nc.scalar.activation(
                hid[h][:, :, 2 * u : 2 * u + 2],
                diffs[u][:, :, H * h : H * (h + 1)].rearrange("p v j -> p j v"),
                ACT.Abs,
            )

        for h in range(2):
            nc.scalar.activation(
                picked[1][:, 1, H * h : H * (h + 1)], boards[3][:].indirect(o5[:, HC * h : HC * (h + 1)]), ACT.Copy
            )
        for t in (1, 0, 2):
            nc.vector.tensor_copy(picked[t // 2][:, t % 2, :], boards[t][:].indirect(o5[:]))
        for h in range(2):
            cols = slice(H * h, H * (h + 1))
            for u in range(2):
                nc.vector.tensor_tensor(diffs[u][:, :, cols], picked[u][:, :, cols], s2[u][:, :, cols], ALU.subtract)
                magnitude(u, h)

        page0 = sb.tile([P, E], F32, name="page0", tag="a3")
        nc.gpsimd.memset(page0[:], 0.0)
        pages = [page0, page1]

        staged = {}
        for h in range(2):
            hid_w = sb.tile([P, H], U32, name="hid_w%d" % h, align_bytes=64)
            hid_s = sb.tile([P, H], U8, name="hid_s%d" % h, align_bytes=64)
            nc.vector.quantize_mx(
                out=hid_w[:].bitcast(E5M2), scales=hid_s[:], in_=hid[h][:].rearrange("p j t -> p (j t)")
            )
            for b in range(N // P):
                cols = slice(P * b, P * (b + 1))
                acc = psum.tile([P, H], F32, name="p%d%d" % (b, h), tag="bank%d" % (2 * h + b))
                nc.tensor.matmul_mx(
                    out=acc[:],
                    lhsT=val_w[:, cols].bitcast(E4M3), lhsT_scale=val_s[:, cols],
                    rhs=hid_w[:].bitcast(E5M2), rhs_scale=hid_s[:],
                    start=True, stop=True,
                )
                staged[b, h] = acc
        p_sb = [sb.tile([P, J], F32, name="p_sb%d" % b) for b in range(N // P)]
        nc.scalar.copy(p_sb[0][:, 0:H], staged[0, 0][:])
        put(False, pages[0], o7[:, 0:HC], p_sb[0][:, 0:H])
        nc.vector.tensor_copy(p_sb[1][:, 0:H], staged[1, 0][:])
        nc.vector.tensor_copy(p_sb[0][:, H:], staged[0, 1][:])
        put(False, pages[0], o7[:, HC:], p_sb[0][:, H:])
        nc.vector.tensor_copy(p_sb[1][:, H:], staged[1, 1][:])
        put(True, pages[1], o7[:], p_sb[1][:])
        for b in range(N // P):
            nc.sync.dma_start(out[P * b : P * (b + 1), :], pages[b][:])
